import numpy as np, ml_dtypes
CORES = [2,3,42,43,82,83,122,123]
N = 8
import mx_ref
BF = ml_dtypes.bfloat16
def entries(a):
    return np.ascontiguousarray(a.T).reshape(-1)
def table(e):
    return np.ascontiguousarray(np.reshape(e, (-1, 16)).T).astype(np.int32)
def cols(t, e):
    v = np.concatenate([t.reshape(128, -1, 4), np.zeros((128, 1, 4), BF)], axis=1)
    return np.ascontiguousarray(v[:, e]).reshape(128, -1)
def cut(t, i, w=512):
    return t[:, w * i:w * i + w]
def f(rng, *shape):
    return mx_ref.flush((rng.standard_normal(shape, dtype=np.float32) * np.exp2(rng.integers(-2, 3, shape[:-1] + (1,)))).astype(BF))
def wide(rng, *shape, cols=0):
    v = rng.standard_normal(shape, dtype=np.float32) * np.exp2(rng.integers(-12, 13, shape)).astype(np.float32)
    if cols: v *= np.repeat(np.exp2(rng.integers(-cols, cols + 1, shape[:-2] + (1, shape[-1] // 4))) * (rng.random(shape[:-2] + (1, shape[-1] // 4)) > 0.0625), 4, axis=-1).astype(np.float32)
    return mx_ref.flush(v.astype(BF))
T, K, O, CAPP = 512, 8, 1, 64
def lists(rng, foreign=False, own=False, same=False, absent=False):
    S = np.full((N, N, CAPP), -1); M = []
    for s in range(N):
        for d in range(N):
            n = CAPP if foreign else rng.integers(1, CAPP + 1)
            if s != d: S[s, d, rng.permutation(CAPP)[:n]] = rng.integers(0, T, n)
    k = np.arange(K)[:, None]
    for r in range(N):
        far = T + np.flatnonzero(S[:, r].reshape(-1) >= 0)
        m = np.where(rng.random((K, T)) < (1.0 if foreign else np.divide(k + 1, K + 1)), rng.choice(far, (K, T)), rng.integers(0, T, (K, T)))
        there = np.zeros((K, T), bool); there[rng.integers(0, K, T), np.arange(T)] = True
        if absent: there.reshape(-1)[rng.permutation(np.flatnonzero(~there))[:K * T - 2 * K * T // 3 - T]] = True
        else: there |= rng.random((K, T)) >= 0.1 + 0.5 * np.divide(k, K - 1)
        m = np.repeat(m[:, :1], T, axis=1) if same else np.where(there, m, -1)
        if own: m = np.stack([rng.permutation(T) for _ in range(K)])
        M.append(table(m))
    return {"send": np.stack([table(S[s]) for s in range(N)]), "mp": np.stack(M)}
def setup_inputs(rng):
    return {"x": f(rng, N, 128, 4 * T), "w": f(rng, N, 128, K * O * 512), **lists(rng)}
def setup_inputs_absent(rng):
    return {**setup_inputs(rng), **lists(rng, absent=True)}
def setup_inputs_foreign(rng):
    return {**setup_inputs(rng), **lists(rng, foreign=True)}
def setup_inputs_same(rng):
    return {**setup_inputs(rng), **lists(rng, same=True)}
def setup_inputs_spread(rng):
    d = setup_inputs(rng); d["x"] = wide(rng, N, 128, 4 * T); return d
def setup_inputs_own(rng):
    return {**setup_inputs(rng), **lists(rng, own=True)}
def check_inputs(d):
    b = []
    for n in ("x", "w"):
        a = np.abs(d[n].astype(np.float32))
        if not np.isfinite(a).all() or ((a > 0) & ((a < 2.0 ** -30) | (a > 2.0 ** 30))).any(): b.append(n)
    for r in range(N):
        s, m = entries(d["send"][r]), entries(d["mp"][r]).reshape(K, T)
        if s.min() < -1 or s.max() >= T or (s[r * CAPP:(r + 1) * CAPP] != -1).any(): b.append("send")
        held = np.concatenate([entries(d["send"][q])[r * CAPP:(r + 1) * CAPP] for q in range(N)])
        if m.min() < -1 or m.max() >= T + N * CAPP or (held[m[m >= T] - T] < 0).any() or (m < 0).all(axis=0).any(): b.append("mp")
    return b
def reference(x, w, send, mp):
    y = np.zeros((N, 128, O * T), np.float32)
    for r in range(N):
        held = [cols(x[s], entries(send[s])[r * CAPP:(r + 1) * CAPP]) for s in range(N)]
        v = np.concatenate([x[r]] + held, axis=1)
        m = entries(mp[r]).reshape(K, T)
        for k in range(K):
            q = mx_ref.quantize(cols(v, m[k]))
            for o in range(O): y[r][:, T * o:T * o + T] += mx_ref.matmul(mx_ref.quantize(cut(w[r], k * O + o)), q)
    return {"y": y}

@@ -1,0 +1,234 @@
+from concourse.bass import DstId, RemoteDMATransfer
+from concourse.mybir import dt, AluOpType, ActivationFunctionType
+
+COLS, MAPS, CAP = 512, 8, 64
+STRIDE = 1028
+WIN = 1 + 2 * COLS
+HALF = COLS // 2
+EARLY = ((0, "S"), (1, "V"), (2, "V"))
+
+SCRATCH = {
+    "xt": ("sbuf", [128, 4 * COLS], "bfloat16"),
+    "wt": ("sbuf", [128, 512 * MAPS], "bfloat16"),
+    "ls": ("sbuf", [128, 32], "int32"),
+    "lm": ("sbuf", [128, 256], "int32"),
+    "offs": ("sbuf", [128, 32], "uint16"),
+    "offm": ("sbuf", [128, 256], "uint16"),
+    "h": ("sbuf", [128, 4 * 7 * CAP], "bfloat16"),
+    "hq": ("sbuf", [128, 7 * CAP], "float8_e4m3fn_x4"),
+    "hp": ("sbuf", [128, 7 * CAP], "uint8"),
+    "xq": ("sbuf", [128, COLS], "float8_e4m3fn_x4"),
+    "xp": ("sbuf", [128, COLS], "uint8"),
+    "wq": ("sbuf", [128, 128 * MAPS], "float8_e4m3fn_x4"),
+    "wp": ("sbuf", [128, 128 * MAPS], "uint8"),
+    "aq": ("sbuf", [128, 7 * CAP], "float8_e4m3fn_x4"),
+    "ap": ("sbuf", [128, 7 * CAP], "uint8"),
+    "win": ("sbuf", [128, STRIDE * MAPS], "float32"),
+    "g0": ("sbuf", [128, COLS], "float32"),
+    "acc": ("sbuf", [128, COLS], "float32"),
+    "ps": ("psum", [128, 512 * MAPS], "float32"),
+}
+SEMAPHORES = ["sl", "sx", "sw0", "sw1", "sw2", "sm", "sy", "cv", "cs", "ct", "arra", "arrb", "loc"]
+
+
+def groups(T, topo, r):
+    me = topo.chip(T.cores[r])
+    far, near, mate = [], [], []
+    for i in range(1, len(T.cores)):
+        s = (r + i) % len(T.cores)
+        c = topo.chip(T.cores[s])
+        if c == me:
+            mate.append(s)
+        elif topo.same_plane(me, c):
+            near.append(s)
+        else:
+            far.append(s)
+    return far, sorted(near), mate
+
+
+def runs(ranks):
+    out = []
+    for i, s in enumerate(ranks):
+        if out and out[-1][1] + out[-1][2] == s:
+            out[-1] = (out[-1][0], out[-1][1], out[-1][2] + 1)
+        else:
+            out.append((i, s, 1))
+    return out
+
+
+def mask_of(engines):
+    m = 0
+    for e in engines:
+        m |= 1 << e
+    return m
+
+
+def rank_program(g, core, T, topo):
+    r = T.rank_of(core)
+    if r is None:
+        return
+    sem = T.sem
+    V, S, P, Y = g.vector, g.scalar, g.tensor, g.sync
+    queue = {"V": V, "S": S, "P": P, "Y": Y, "G": g}
+    Copy = ActivationFunctionType.Copy
+    cnt = {"cv": 0, "cs": 0, "ct": 0}
+    seen = {}
+
+    def wait(name, s, n):
+        if seen.get((name, s), 0) < n:
+            queue[name].wait_ge(sem[s], n)
+            seen[(name, s)] = n
+
+    def inc(s, call):
+        call.then_inc(sem[s], 1)
+        cnt[s] += 1
+        return s, cnt[s]
+
+    far, near, mate = groups(T, topo, r)
+    dests = far + near + mate
+    cut = len(far) // 2
+    first = sorted(far + mate)
+    order = first + near
+
+    for i in range(4):
+        Y.dma_start(T.ls[16 * i:16 * i + 16, :], T.send[:, :]).then_inc(sem.sl, 16)
+        S.dma_start(T.ls[64 + 16 * i:80 + 16 * i, :], T.send[:, :]).then_inc(sem.sl, 16)
+    Y.dma_start(T.xt[:, 0:1024], T.x[:, 0:1024]).then_inc(sem.sx, 16)
+    S.dma_start(T.xt[:, 1024:2048], T.x[:, 1024:2048]).then_inc(sem.sx, 16)
+    wparts = ((0, 2), (2, 4), (4, 8))
+    for i, (a, b) in enumerate(wparts):
+        Y.dma_start(T.wt[:, 512 * a:512 * b], T.w[:, 512 * a:512 * b]).then_inc(sem["sw%d" % i], 16)
+    for i in range(8):
+        Y.dma_start(T.lm[16 * i:16 * i + 16, :], T.mp[:, :]).then_inc(sem.sm, 16)
+
+    for k in range(MAPS):
+        inc("cv", V.memset(T.win[:, k * STRIDE:k * STRIDE + 1], 0.0))
+        o = k * STRIDE + 1 + COLS + CAP * r
+        zeros = inc("cv", V.memset(T.win[:, o:o + CAP], 0.0))
+
+    wait("V", "sl", 128)
+    for i, d, n in runs(dests):
+        offs = inc("cv", V.tensor_scalar(T.offs[:, 4 * i:4 * (i + n)], T.ls[:, 4 * d:4 * (d + n)], 4.0, 0.0,
+                                         AluOpType.mult, AluOpType.max))
+
+    def gather(name, lo, hi, t):
+        wait(name, *offs)
+        wait(name, "sx", 32)
+        out = T.h[:, 4 * lo + t:4 * hi:4]
+        src = T.xt[:, t:4 * COLS].indirect(T.offs[:, lo // 16:hi // 16])
+        if name == "V":
+            return inc("cv", V.tensor_copy(out, src))
+        return inc("cs", S.activation(out, src, Copy))
+
+    def pack(lo, hi, parts):
+        for p in parts:
+            wait("V", *p)
+        return inc("cv", V.quantize_mx(T.hq[:, lo:hi], T.hp[:, lo:hi], T.h[:, 4 * lo:4 * hi]))
+
+    def pack_w(i):
+        a, b = wparts[i]
+        wait("V", "sw%d" % i, 16)
+        n = inc("cv", V.quantize_mx(T.wq[:, 128 * a:128 * b], T.wp[:, 128 * a:128 * b], T.wt[:, 512 * a:512 * b]))
+        return {k: n for k in range(a, b)}
+
+    b1, b2, b3 = CAP * cut, CAP * len(far), CAP * len(dests)
+    parts = [gather("V", 0, b1, 0), gather("V", 0, b1, 1), gather("S", 0, b1, 2), gather("S", 0, b1, 3)]
+    packed1 = pack(0, b1, parts)
+    parts = [gather("V", b1, b2, 0), gather("V", b1, b2, 1), gather("S", b1, b2, 2), gather("S", b1, b2, 3)]
+    packed2 = pack(b1, b2, parts)
+    parts = [gather("V", b2, b3, 0)] + [gather("S", b2, b3, t) for t in (1, 2, 3)]
+    xq = inc("cv", V.quantize_mx(T.xq[:, :], T.xp[:, :], T.xt[:, :]))
+    packed3 = pack(b2, b3, parts)
+    wq = pack_w(0)
+    wq.update(pack_w(1))
+    wq.update(pack_w(2))
+    wait("V", "sm", 128)
+    offm = inc("cv", V.tensor_scalar(T.offm[:, :], T.lm[:, :], 1.0, None, AluOpType.add))
+
+    out_engines = topo.engines(core, T.cores[far[0]])
+    home_engines = [e for e in topo.engines(core, T.cores[mate[0]]) if e not in out_engines][:2]
+
+    def transfer(d, engines, codes):
+        dfar, dnear, dmate = groups(T, topo, d)
+        rid, pid, _ = topo.addr(T.cores[d])
+        a = CAP * dests.index(d)
+        p = CAP * (sorted(dfar + dmate) + dnear).index(r)
+        if codes:
+            src, dst = T.hq[:, a:a + CAP].bitcast(dt.uint8), T.aq[:, p:p + CAP].bitcast(dt.uint8)
+        else:
+            src, dst = T.hp[:, a:a + CAP], T.ap[:, p:p + CAP]
+        return RemoteDMATransfer(dst_ids=[DstId(rid=rid, pnc=pid)], dma_engine_mask=mask_of(engines),
+                                 remote_sem=sem.arrb if r in dnear else sem.arra, src=src, dst=dst)
+
+    local, comes_a, comes_b = 0, 0, 0
+    for ranks, home, codes, packed in ((far[:cut], [], True, packed1), (far[cut:], [], True, packed2),
+                                       (far, [], False, packed2), (near, mate, True, packed3),
+                                       (near, mate, False, packed3)):
+        wait("G", *packed)
+        n = len(out_engines) // len(ranks)
+        tr = [transfer(d, out_engines[n * i:n * i + n], codes) for i, d in enumerate(ranks)]
+        tr += [transfer(d, home_engines, codes) for d in home]
+        g.remote_dma_fused(tr, local_sem=sem.loc)
+        local += n * len(ranks) + len(home_engines) * len(home)
+        if home:
+            comes_b += n * len(ranks)
+            comes_a += len(home_engines) * len(home)
+        else:
+            comes_a += n * len(ranks)
+
+    def product(k, bank, q, p, a, b):
+        return inc("ct", P.matmul_mx(T.ps[:, 512 * bank:512 * bank + b - a], T.wq[:, 128 * k:128 * k + 128],
+                                     T.wp[:, 128 * k:128 * k + 128], q[:, a:b], p[:, a:b], True, True))
+
+    full = {k: [offm, zeros] for k in range(MAPS)}
+
+    def copy(name, m, k, bank, a, to, n):
+        wait(name, *m)
+        dst, src = T.win[:, k * STRIDE + to:k * STRIDE + to + n], T.ps[:, 512 * bank + a:512 * bank + a + n]
+        done = inc("cv", V.tensor_copy(dst, src)) if name == "V" else inc("cs", S.activation(dst, src, Copy))
+        full[k].append(done)
+        return done
+
+    def copy_slots(name, m, k, bank, ranks):
+        for i, s, n in runs(ranks):
+            done = copy(name, m, k, bank, CAP * i, 1 + COLS + CAP * s, CAP * n)
+        return done
+
+    free = {}
+    for k in range(MAPS):
+        wait("P", *xq)
+        wait("P", *wq[k])
+        m = product(k, k, T.xq, T.xp, 0, COLS)
+        free[k] = copy("V" if k in (3, 5, 7) else "S", m, k, k, 0, 1, COLS)
+    na = CAP * len(first)
+    wait("P", "arra", comes_a)
+    for k, name in EARLY:
+        wait("P", *free[k])
+        copy_slots(name, product(k, k, T.aq, T.ap, 0, na), k, k, first)
+    wait("P", "arrb", comes_b)
+    for k, name in EARLY:
+        bank = MAPS - len(EARLY) + k
+        wait("P", *free[bank])
+        free[bank] = copy_slots(name, product(k, bank, T.aq, T.ap, na, b3), k, bank, near)
+
+    def pick(name, k, c):
+        for need in full[k]:
+            wait(name, *need)
+        o = 32 * k + 16 * c
+        return T.win[:, k * STRIDE:k * STRIDE + WIN].indirect(T.offm[:, o:o + 16])
+
+    halves = [slice(0, HALF), slice(HALF, COLS)]
+    acc = [inc("cs", S.activation(T.g0[:, halves[c]], pick("S", 0, c), Copy)) for c in range(2)]
+    for k in range(len(EARLY), MAPS):
+        wait("P", *free[k])
+        copy_slots("S", product(k, k, T.aq, T.ap, 0, b3), k, k, order)
+    for k in range(1, MAPS):
+        other = T.g0 if k == 1 else T.acc
+        for c in range(2):
+            wait("V", *acc[c])
+            acc[c] = inc("cv", V.tensor_tensor(T.acc[:, halves[c]], pick("V", k, c), other[:, halves[c]], AluOpType.add))
+    for c, name in ((0, "Y"), (1, "S")):
+        wait(name, *acc[c])
+        queue[name].dma_start(T.y[:, halves[c]], T.acc[:, halves[c]]).then_inc(sem.sy, 16)
+    wait("G", "loc", local)
+    Y.wait_ge(sem.sy, 32)

@@ -4,8 +4,32 @@ from concourse.mybir import dt, AluOpType, ActivationFunctionType
 COLS, MAPS, CAP = 512, 8, 64
 STRIDE = 1028
 WIN = 1 + 2 * COLS
-HALF = COLS // 2
-EARLY = ((0, "S"), (1, "V"), (2, "V"))
+WPARTS = ((0, 1), (2, 3), (4, 5, 6, 7))
+
+BLOCKS = ((("nb", "f1a"), "VVSS"), (("f1b", "f2a"), "VVSS"), (("f2b", "na", "m"), "VSSS"))
+RELAYED = ("nb",)
+LATE = ("nb", "f2b", "na")
+HELPER = {"scales": slice(1, 4, 2), "codes": slice(0, 8, 2)}
+CALLS = (
+    ("scales", (("nb", "home", 0, 8, 2),)),
+    ("codes", (("nb", "home", 0, 8, 2), ("f1a", "out", 0, 8, 2))),
+    ("codes", (("f1b", "out", 1, 8, 2), ("f2a", "out", 0, 8, 2))),
+    ("scales", (("f1a", "out", 1, 4, 2), ("f1b", "out", 5, 8, 2), ("f2a", "out", 0, 8, 2))),
+    ("codes", (("f2b", "out", 0, 8, 2), ("na", "out", 1, 8, 2), ("m", "home", 0, 8, 2))),
+    ("scales", (("f2b", "out", 0, 8, 2), ("na", "out", 1, 8, 2), ("m", "home", 0, 8, 2))),
+)
+PLAN = (
+    ("gather", 1), ("pack", 1), ("gather", 2), ("x",), ("w", 0), ("pack", 2),
+    ("x", 0, "S"), ("offm", 0), ("w", 1), ("offm", 32), ("x", 1, "S"), ("x", 2, "S"), ("w", 2), ("offm", 64),
+    ("x", 3, "S"), ("x", 4, "V"), ("x", 5, "S"), ("x", 6, "V"),
+    ("early", 0, "S"), ("early", 1, "V"), ("early", 2, "V"),
+    ("late", 0, "S"), ("late", 1, "V"), ("late", 2, "V"),
+    ("pick", 0, 0, 256), ("pick", 0, 256, 512),
+    ("all", 3, "S"), ("all", 4, "S"), ("all", 5, "S"), ("all", 6, "S"), ("x", 7, "S"), ("all", 7, "S"),
+) + tuple(("add", k, a, a + 256) for k in range(1, MAPS - 1) for a in (0, 256)) + (
+    ("add", 7, 0, 256), ("store", "Y", 0, 256), ("add", 7, 256, 384), ("store", "S", 256, 384),
+    ("add", 7, 384, 512), ("store", "Y", 384, 512),
+)
 
 SCRATCH = {
     "xt": ("sbuf", [128, 4 * COLS], "bfloat16"),
@@ -23,15 +47,17 @@ SCRATCH = {
     "wp": ("sbuf", [128, 128 * MAPS], "uint8"),
     "aq": ("sbuf", [128, 7 * CAP], "float8_e4m3fn_x4"),
     "ap": ("sbuf", [128, 7 * CAP], "uint8"),
+    "rq": ("sbuf", [128, CAP], "float8_e4m3fn_x4"),
+    "rp": ("sbuf", [128, CAP], "uint8"),
     "win": ("sbuf", [128, STRIDE * MAPS], "float32"),
     "g0": ("sbuf", [128, COLS], "float32"),
     "acc": ("sbuf", [128, COLS], "float32"),
     "ps": ("psum", [128, 512 * MAPS], "float32"),
 }
-SEMAPHORES = ["sl", "sx", "sw0", "sw1", "sw2", "sm", "sy", "cv", "cs", "ct", "arra", "arrb", "loc"]
+SEMAPHORES = ["sl", "sx", "sw0", "sw1", "sw2", "sm", "sy", "cv", "cs", "ct", "early", "late", "codes", "scales", "loc"]
 
 
-def groups(T, topo, r):
+def pieces(T, topo, r):
     me = topo.chip(T.cores[r])
     far, near, mate = [], [], []
     for i in range(1, len(T.cores)):
@@ -43,7 +69,31 @@ def groups(T, topo, r):
             near.append(s)
         else:
             far.append(s)
-    return far, sorted(near), mate
+    i = int(r > mate[0])
+    if not i:
+        far.reverse()
+    to = {"m": mate[0]}
+    for name, pair in (("f1", far[:2]), ("f2", far[2:]), ("n", near)):
+        to[name + "a"], to[name + "b"] = sorted(pair)[1 - i], sorted(pair)[i]
+    return to
+
+
+def helpers(T, topo, r):
+    to, core = pieces(T, topo, r), T.cores[r]
+    free = [c for c in topo.cores_of(core) if topo.die(c) != topo.die(core)]
+    out = {}
+    for name in RELAYED:
+        able = [c for c in free if topo.may_write(c, T.cores[to[name]])][:2]
+        out[name] = able[int(r > to["m"])]
+        free = [c for c in free if c not in able]
+    return out
+
+
+def senders(T, topo, r):
+    n = len(T.cores)
+    late = [s % n for s in range(r + 1, r + n) if r in [pieces(T, topo, s % n)[name] for name in LATE]]
+    early = [s % n for s in range(r - n // 2, r + n // 2) if s != r and s % n not in late]
+    return {"early": early, "late": late}
 
 
 def runs(ranks):
@@ -56,16 +106,42 @@ def runs(ranks):
     return out
 
 
-def mask_of(engines):
-    m = 0
-    for e in engines:
-        m |= 1 << e
-    return m
+def view(q, p, a, kind):
+    return q[:, a:a + CAP].bitcast(dt.uint8) if kind == "codes" else p[:, a:a + CAP]
+
+
+def write(topo, core, engines, src, dst, arrived):
+    rid, pid, _ = topo.addr(core)
+    return RemoteDMATransfer(dst_ids=[DstId(rid=rid, pnc=pid)], dma_engine_mask=sum(1 << e for e in engines),
+                             remote_sem=arrived, src=src, dst=dst)
+
+
+def deliver(T, topo, r, name, engines, src, kind):
+    d = pieces(T, topo, r)[name]
+    came = senders(T, topo, d)
+    dst = view(T.aq, T.ap, CAP * (came["early"] + came["late"]).index(r), kind)
+    return write(topo, T.cores[d], engines, src, dst, T.sem.late if name in LATE else T.sem.early)
+
+
+def helper_program(g, core, T, topo, r, name):
+    out, local = topo.engines(core, T.cores[pieces(T, topo, r)[name]]), 0
+    for kind, parts in CALLS:
+        for piece, _, a, b, step in parts:
+            if piece == name:
+                engines = out[HELPER[kind]]
+                g.wait_ge(T.sem[kind], len(range(a, b, step)))
+                g.remote_dma_fused([deliver(T, topo, r, name, engines, view(T.rq, T.rp, 0, kind), kind)], local_sem=T.sem.loc)
+                local += len(engines)
+    g.wait_ge(T.sem.loc, local)
 
 
 def rank_program(g, core, T, topo):
     r = T.rank_of(core)
     if r is None:
+        for s in range(len(T.cores)):
+            for name, c in helpers(T, topo, s).items():
+                if c == core:
+                    helper_program(g, core, T, topo, s, name)
         return
     sem = T.sem
     V, S, P, Y = g.vector, g.scalar, g.tensor, g.sync
@@ -84,151 +160,156 @@ def rank_program(g, core, T, topo):
         cnt[s] += 1
         return s, cnt[s]
 
-    far, near, mate = groups(T, topo, r)
-    dests = far + near + mate
-    cut = len(far) // 2
-    first = sorted(far + mate)
-    order = first + near
+    to, helper, came = pieces(T, topo, r), helpers(T, topo, r), senders(T, topo, r)
+    came["all"] = came["early"] + came["late"]
+    names = [name for block, _ in BLOCKS for name in sorted(block, key=to.get)]
+    done = {}
 
-    for i in range(4):
-        Y.dma_start(T.ls[16 * i:16 * i + 16, :], T.send[:, :]).then_inc(sem.sl, 16)
-        S.dma_start(T.ls[64 + 16 * i:80 + 16 * i, :], T.send[:, :]).then_inc(sem.sl, 16)
-    Y.dma_start(T.xt[:, 0:1024], T.x[:, 0:1024]).then_inc(sem.sx, 16)
-    S.dma_start(T.xt[:, 1024:2048], T.x[:, 1024:2048]).then_inc(sem.sx, 16)
-    wparts = ((0, 2), (2, 4), (4, 8))
-    for i, (a, b) in enumerate(wparts):
-        Y.dma_start(T.wt[:, 512 * a:512 * b], T.w[:, 512 * a:512 * b]).then_inc(sem["sw%d" % i], 16)
-    for i in range(8):
+    for i, q in enumerate((Y, S)):
+        q.dma_start(T.ls[16 * i:16 * i + 16, :], T.send[:, :]).then_inc(sem.sl, 16)
+    Y.dma_start(T.xt[:, :], T.x[:, :]).then_inc(sem.sx, 16)
+    for i in range(2):
         Y.dma_start(T.lm[16 * i:16 * i + 16, :], T.mp[:, :]).then_inc(sem.sm, 16)
+    for i, maps in enumerate(WPARTS):
+        a, b = 512 * maps[0], 512 * (maps[-1] + 1)
+        Y.dma_start(T.wt[:, a:b], T.w[:, a:b]).then_inc(sem["sw%d" % i], 16)
 
+    inc("cv", V.memset(T.win[:, 0:STRIDE * MAPS:STRIDE], 0.0))
     for k in range(MAPS):
-        inc("cv", V.memset(T.win[:, k * STRIDE:k * STRIDE + 1], 0.0))
         o = k * STRIDE + 1 + COLS + CAP * r
         zeros = inc("cv", V.memset(T.win[:, o:o + CAP], 0.0))
 
-    wait("V", "sl", 128)
-    for i, d, n in runs(dests):
-        offs = inc("cv", V.tensor_scalar(T.offs[:, 4 * i:4 * (i + n)], T.ls[:, 4 * d:4 * (d + n)], 4.0, 0.0,
+    wait("V", "sl", 32)
+    for i, d, n in runs([to[name] for name in names]):
+        offs = inc("cv", V.tensor_scalar(T.offs[0:32, 4 * i:4 * (i + n)], T.ls[0:32, 4 * d:4 * (d + n)], 4.0, 0.0,
                                          AluOpType.mult, AluOpType.max))
+    wait("V", *offs)
+    for p in (32, 64, 96):
+        offs = inc("cv", V.tensor_copy(T.offs[p:p + 32, 0:28], T.offs[0:32, 0:28]))
 
-    def gather(name, lo, hi, t):
-        wait(name, *offs)
-        wait(name, "sx", 32)
-        out = T.h[:, 4 * lo + t:4 * hi:4]
-        src = T.xt[:, t:4 * COLS].indirect(T.offs[:, lo // 16:hi // 16])
-        if name == "V":
-            return inc("cv", V.tensor_copy(out, src))
-        return inc("cs", S.activation(out, src, Copy))
+    def span(b):
+        lo = CAP * sum(len(block) for block, _ in BLOCKS[:b])
+        return lo, lo + CAP * len(BLOCKS[b][0])
 
-    def pack(lo, hi, parts):
-        for p in parts:
-            wait("V", *p)
-        return inc("cv", V.quantize_mx(T.hq[:, lo:hi], T.hp[:, lo:hi], T.h[:, 4 * lo:4 * hi]))
+    def gather(b):
+        lo, hi = span(b)
+        done["rows", b] = []
+        for t, name in enumerate(BLOCKS[b][1]):
+            wait(name, *offs)
+            wait(name, "sx", 16)
+            out = T.h[:, 4 * lo + t:4 * hi:4]
+            src = T.xt[:, t:4 * COLS].indirect(T.offs[:, lo // 16:hi // 16])
+            done["rows", b].append(inc("cv", V.tensor_copy(out, src)) if name == "V"
+                                   else inc("cs", S.activation(out, src, Copy)))
+
+    def pack(b):
+        lo, hi = span(b)
+        for rows in done["rows", b]:
+            wait("V", *rows)
+        n = inc("cv", V.quantize_mx(T.hq[:, lo:hi], T.hp[:, lo:hi], T.h[:, 4 * lo:4 * hi]))
+        done.update({name: n for name in BLOCKS[b][0]})
 
     def pack_w(i):
-        a, b = wparts[i]
+        a, b = WPARTS[i][0], WPARTS[i][-1] + 1
         wait("V", "sw%d" % i, 16)
         n = inc("cv", V.quantize_mx(T.wq[:, 128 * a:128 * b], T.wp[:, 128 * a:128 * b], T.wt[:, 512 * a:512 * b]))
-        return {k: n for k in range(a, b)}
+        done.update({("w", k): n for k in WPARTS[i]})
 
-    b1, b2, b3 = CAP * cut, CAP * len(far), CAP * len(dests)
-    parts = [gather("V", 0, b1, 0), gather("V", 0, b1, 1), gather("S", 0, b1, 2), gather("S", 0, b1, 3)]
-    packed1 = pack(0, b1, parts)
-    parts = [gather("V", b1, b2, 0), gather("V", b1, b2, 1), gather("S", b1, b2, 2), gather("S", b1, b2, 3)]
-    packed2 = pack(b1, b2, parts)
-    parts = [gather("V", b2, b3, 0)] + [gather("S", b2, b3, t) for t in (1, 2, 3)]
-    xq = inc("cv", V.quantize_mx(T.xq[:, :], T.xp[:, :], T.xt[:, :]))
-    packed3 = pack(b2, b3, parts)
-    wq = pack_w(0)
-    wq.update(pack_w(1))
-    wq.update(pack_w(2))
-    wait("V", "sm", 128)
-    offm = inc("cv", V.tensor_scalar(T.offm[:, :], T.lm[:, :], 1.0, None, AluOpType.add))
+    out = topo.engines(core, T.cores[to["f1a"]])
+    comes = {"early": 0, "late": 0}
+    for kind, parts in CALLS:
+        for name, _, a, b, step in parts:
+            comes["late" if name in LATE else "early"] += len(out[HELPER[kind]] if name in RELAYED else out[a:b:step])
 
-    out_engines = topo.engines(core, T.cores[far[0]])
-    home_engines = [e for e in topo.engines(core, T.cores[mate[0]]) if e not in out_engines][:2]
+    full = {k: [zeros] for k in range(MAPS)}
+    banks = []
 
-    def transfer(d, engines, codes):
-        dfar, dnear, dmate = groups(T, topo, d)
-        rid, pid, _ = topo.addr(T.cores[d])
-        a = CAP * dests.index(d)
-        p = CAP * (sorted(dfar + dmate) + dnear).index(r)
-        if codes:
-            src, dst = T.hq[:, a:a + CAP].bitcast(dt.uint8), T.aq[:, p:p + CAP].bitcast(dt.uint8)
+    def fill(what, k, name):
+        bank = len(banks) % MAPS
+        if len(banks) >= MAPS:
+            wait("P", *banks[len(banks) - MAPS])
+        wait("P", *done["w", k])
+        if what == "x":
+            wait("P", *done["x"])
+            q, p, a, b, cuts = T.xq, T.xp, 0, COLS, [(0, 1, COLS)]
         else:
-            src, dst = T.hp[:, a:a + CAP], T.ap[:, p:p + CAP]
-        return RemoteDMATransfer(dst_ids=[DstId(rid=rid, pnc=pid)], dma_engine_mask=mask_of(engines),
-                                 remote_sem=sem.arrb if r in dnear else sem.arra, src=src, dst=dst)
-
-    local, comes_a, comes_b = 0, 0, 0
-    for ranks, home, codes, packed in ((far[:cut], [], True, packed1), (far[cut:], [], True, packed2),
-                                       (far, [], False, packed2), (near, mate, True, packed3),
-                                       (near, mate, False, packed3)):
-        wait("G", *packed)
-        n = len(out_engines) // len(ranks)
-        tr = [transfer(d, out_engines[n * i:n * i + n], codes) for i, d in enumerate(ranks)]
-        tr += [transfer(d, home_engines, codes) for d in home]
-        g.remote_dma_fused(tr, local_sem=sem.loc)
-        local += n * len(ranks) + len(home_engines) * len(home)
-        if home:
-            comes_b += n * len(ranks)
-            comes_a += len(home_engines) * len(home)
-        else:
-            comes_a += n * len(ranks)
-
-    def product(k, bank, q, p, a, b):
-        return inc("ct", P.matmul_mx(T.ps[:, 512 * bank:512 * bank + b - a], T.wq[:, 128 * k:128 * k + 128],
-                                     T.wp[:, 128 * k:128 * k + 128], q[:, a:b], p[:, a:b], True, True))
-
-    full = {k: [offm, zeros] for k in range(MAPS)}
-
-    def copy(name, m, k, bank, a, to, n):
+            for arr in ("early", "late"):
+                if what in (arr, "all"):
+                    wait("P", arr, comes[arr])
+            a = CAP * came["all"].index(came[what][0])
+            q, p, b = T.aq, T.ap, a + CAP * len(came[what])
+            cuts = [(CAP * i, 1 + COLS + CAP * s, CAP * n) for i, s, n in runs(came[what])]
+        w = slice(128 * k, 128 * k + 128)
+        m = inc("ct", P.matmul_mx(T.ps[:, 512 * bank:512 * bank + b - a], T.wq[:, w], T.wp[:, w],
+                                  q[:, a:b], p[:, a:b], True, True))
         wait(name, *m)
-        dst, src = T.win[:, k * STRIDE + to:k * STRIDE + to + n], T.ps[:, 512 * bank + a:512 * bank + a + n]
-        done = inc("cv", V.tensor_copy(dst, src)) if name == "V" else inc("cs", S.activation(dst, src, Copy))
-        full[k].append(done)
-        return done
+        for a, at, n in cuts:
+            dst, src = T.win[:, k * STRIDE + at:k * STRIDE + at + n], T.ps[:, 512 * bank + a:512 * bank + a + n]
+            last = inc("cv", V.tensor_copy(dst, src)) if name == "V" else inc("cs", S.activation(dst, src, Copy))
+        full[k].append(last)
+        banks.append(last)
 
-    def copy_slots(name, m, k, bank, ranks):
-        for i, s, n in runs(ranks):
-            done = copy(name, m, k, bank, CAP * i, 1 + COLS + CAP * s, CAP * n)
-        return done
-
-    free = {}
-    for k in range(MAPS):
-        wait("P", *xq)
-        wait("P", *wq[k])
-        m = product(k, k, T.xq, T.xp, 0, COLS)
-        free[k] = copy("V" if k in (3, 5, 7) else "S", m, k, k, 0, 1, COLS)
-    na = CAP * len(first)
-    wait("P", "arra", comes_a)
-    for k, name in EARLY:
-        wait("P", *free[k])
-        copy_slots(name, product(k, k, T.aq, T.ap, 0, na), k, k, first)
-    wait("P", "arrb", comes_b)
-    for k, name in EARLY:
-        bank = MAPS - len(EARLY) + k
-        wait("P", *free[bank])
-        free[bank] = copy_slots(name, product(k, bank, T.aq, T.ap, na, b3), k, bank, near)
-
-    def pick(name, k, c):
+    def pick(name, k, a, b):
+        wait(name, *done["offm"])
         for need in full[k]:
             wait(name, *need)
-        o = 32 * k + 16 * c
-        return T.win[:, k * STRIDE:k * STRIDE + WIN].indirect(T.offm[:, o:o + 16])
+        return T.win[:, k * STRIDE:k * STRIDE + WIN].indirect(T.offm[:, 32 * k + a // 16:32 * k + b // 16])
 
-    halves = [slice(0, HALF), slice(HALF, COLS)]
-    acc = [inc("cs", S.activation(T.g0[:, halves[c]], pick("S", 0, c), Copy)) for c in range(2)]
-    for k in range(len(EARLY), MAPS):
-        wait("P", *free[k])
-        copy_slots("S", product(k, k, T.aq, T.ap, 0, b3), k, k, order)
-    for k in range(1, MAPS):
-        other = T.g0 if k == 1 else T.acc
-        for c in range(2):
-            wait("V", *acc[c])
-            acc[c] = inc("cv", V.tensor_tensor(T.acc[:, halves[c]], pick("V", k, c), other[:, halves[c]], AluOpType.add))
-    for c, name in ((0, "Y"), (1, "S")):
-        wait(name, *acc[c])
-        queue[name].dma_start(T.y[:, halves[c]], T.acc[:, halves[c]]).then_inc(sem.sy, 16)
+    def summed(name, a, b):
+        for c in range(a, b, 128):
+            wait(name, *done["sum", c])
+
+    stores = 0
+
+    gather(0)
+    pack(0)
+    for step in PLAN:
+        if step[0] == "gather":
+            gather(step[1])
+        elif step[0] == "pack":
+            pack(step[1])
+        elif step == ("x",):
+            done["x"] = inc("cv", V.quantize_mx(T.xq[:, :], T.xp[:, :], T.xt[:, :]))
+        elif step[0] == "w":
+            pack_w(step[1])
+        elif step[0] == "offm":
+            n = step[1]
+            if n == 0:
+                wait("V", "sm", 32)
+                done["offm"] = inc("cv", V.tensor_scalar(T.offm[0:32, :], T.lm[0:32, :], 1.0, None, AluOpType.add))
+            else:
+                wait("V", *done["offm"])
+                done["offm"] = inc("cv", V.tensor_copy(T.offm[n:2 * n, :], T.offm[0:n, :]))
+        elif step[0] == "pick":
+            _, k, a, b = step
+            last = inc("cs", S.activation(T.g0[:, a:b], pick("S", k, a, b), Copy))
+            done.update({("sum", c): last for c in range(a, b, 128)})
+        elif step[0] == "add":
+            _, k, a, b = step
+            other = T.g0 if done["sum", a][0] == "cs" else T.acc
+            summed("V", a, b)
+            last = inc("cv", V.tensor_tensor(T.acc[:, a:b], pick("V", k, a, b), other[:, a:b], AluOpType.add))
+            done.update({("sum", c): last for c in range(a, b, 128)})
+        elif step[0] == "store":
+            _, name, a, b = step
+            summed(name, a, b)
+            queue[name].dma_start(T.y[:, a:b], T.acc[:, a:b]).then_inc(sem.sy, 16)
+            stores += 16
+        else:
+            fill(*step)
+
+    sets = {"out": out, "home": [e for e in topo.engines(core, T.cores[to["m"]]) if e not in out]}
+    local = 0
+    for kind, parts in CALLS:
+        transfers = []
+        for name, which, a, b, step in parts:
+            wait("G", *done[name])
+            engines, src = sets[which][a:b:step], view(T.hq, T.hp, CAP * names.index(name), kind)
+            local += len(engines)
+            if name in RELAYED:
+                transfers.append(write(topo, helper[name], engines, src, view(T.rq, T.rp, 0, kind), sem[kind]))
+            else:
+                transfers.append(deliver(T, topo, r, name, engines, src, kind))
+        g.remote_dma_fused(transfers, local_sem=sem.loc)
     wait("G", "loc", local)
-    Y.wait_ge(sem.sy, 32)
+    Y.wait_ge(sem.sy, stores)

from concourse.bass import DstId, RemoteDMATransfer
from concourse.mybir import dt, AluOpType, ActivationFunctionType

COLS, MAPS, CAP = 512, 8, 64
STRIDE = 1028
WIN = 1 + 2 * COLS
WPARTS = ((0, 1), (2, 3), (4, 5, 6, 7))

BLOCKS = ((("nb", "f1a"), "VVSS"), (("f1b", "f2a"), "VVSS"), (("f2b", "na", "m"), "VSSS"))
RELAYED = ("nb",)
LATE = ("nb", "f2b", "na")
HELPER = {"scales": slice(1, 4, 2), "codes": slice(0, 8, 2)}
CALLS = (
    ("scales", (("nb", "home", 0, 8, 2),)),
    ("codes", (("nb", "home", 0, 8, 2), ("f1a", "out", 0, 8, 2))),
    ("codes", (("f1b", "out", 1, 8, 2), ("f2a", "out", 0, 8, 2))),
    ("scales", (("f1a", "out", 1, 4, 2), ("f1b", "out", 5, 8, 2), ("f2a", "out", 0, 8, 2))),
    ("codes", (("f2b", "out", 0, 8, 2), ("na", "out", 1, 8, 2), ("m", "home", 0, 8, 2))),
    ("scales", (("f2b", "out", 0, 8, 2), ("na", "out", 1, 8, 2), ("m", "home", 0, 8, 2))),
)
PLAN = (
    ("gather", 1), ("pack", 1), ("gather", 2), ("x",), ("w", 0), ("pack", 2),
    ("x", 0, "S"), ("offm", 0), ("w", 1), ("offm", 32), ("x", 1, "S"), ("x", 2, "S"), ("w", 2), ("offm", 64),
    ("x", 3, "S"), ("x", 4, "V"), ("x", 5, "S"), ("x", 6, "V"),
    ("early", 0, "S"), ("early", 1, "V"), ("early", 2, "V"),
    ("late", 0, "S"), ("late", 1, "V"), ("late", 2, "V"),
    ("pick", 0, 0, 256), ("pick", 0, 256, 512),
    ("all", 3, "S"), ("all", 4, "S"), ("all", 5, "S"), ("all", 6, "S"), ("x", 7, "S"), ("all", 7, "S"),
) + tuple(("add", k, a, a + 256) for k in range(1, MAPS - 1) for a in (0, 256)) + (
    ("add", 7, 0, 256), ("store", "Y", 0, 256), ("add", 7, 256, 384), ("store", "S", 256, 384),
    ("add", 7, 384, 512), ("store", "Y", 384, 512),
)

SCRATCH = {
    "xt": ("sbuf", [128, 4 * COLS], "bfloat16"),
    "wt": ("sbuf", [128, 512 * MAPS], "bfloat16"),
    "ls": ("sbuf", [128, 32], "int32"),
    "lm": ("sbuf", [128, 256], "int32"),
    "offs": ("sbuf", [128, 32], "uint16"),
    "offm": ("sbuf", [128, 256], "uint16"),
    "h": ("sbuf", [128, 4 * 7 * CAP], "bfloat16"),
    "hq": ("sbuf", [128, 7 * CAP], "float8_e4m3fn_x4"),
    "hp": ("sbuf", [128, 7 * CAP], "uint8"),
    "xq": ("sbuf", [128, COLS], "float8_e4m3fn_x4"),
    "xp": ("sbuf", [128, COLS], "uint8"),
    "wq": ("sbuf", [128, 128 * MAPS], "float8_e4m3fn_x4"),
    "wp": ("sbuf", [128, 128 * MAPS], "uint8"),
    "aq": ("sbuf", [128, 7 * CAP], "float8_e4m3fn_x4"),
    "ap": ("sbuf", [128, 7 * CAP], "uint8"),
    "rq": ("sbuf", [128, CAP], "float8_e4m3fn_x4"),
    "rp": ("sbuf", [128, CAP], "uint8"),
    "win": ("sbuf", [128, STRIDE * MAPS], "float32"),
    "g0": ("sbuf", [128, COLS], "float32"),
    "acc": ("sbuf", [128, COLS], "float32"),
    "ps": ("psum", [128, 512 * MAPS], "float32"),
}
SEMAPHORES = ["sl", "sx", "sw0", "sw1", "sw2", "sm", "sy", "cv", "cs", "ct", "early", "late", "codes", "scales", "loc"]


def pieces(T, topo, r):
    me = topo.chip(T.cores[r])
    far, near, mate = [], [], []
    for i in range(1, len(T.cores)):
        s = (r + i) % len(T.cores)
        c = topo.chip(T.cores[s])
        if c == me:
            mate.append(s)
        elif topo.same_plane(me, c):
            near.append(s)
        else:
            far.append(s)
    i = int(r > mate[0])
    if not i:
        far.reverse()
    to = {"m": mate[0]}
    for name, pair in (("f1", far[:2]), ("f2", far[2:]), ("n", near)):
        to[name + "a"], to[name + "b"] = sorted(pair)[1 - i], sorted(pair)[i]
    return to


def helpers(T, topo, r):
    to, core = pieces(T, topo, r), T.cores[r]
    free = [c for c in topo.cores_of(core) if topo.die(c) != topo.die(core)]
    out = {}
    for name in RELAYED:
        able = [c for c in free if topo.may_write(c, T.cores[to[name]])][:2]
        out[name] = able[int(r > to["m"])]
        free = [c for c in free if c not in able]
    return out


def senders(T, topo, r):
    n = len(T.cores)
    late = [s % n for s in range(r + 1, r + n) if r in [pieces(T, topo, s % n)[name] for name in LATE]]
    early = [s % n for s in range(r - n // 2, r + n // 2) if s != r and s % n not in late]
    return {"early": early, "late": late}


def runs(ranks):
    out = []
    for i, s in enumerate(ranks):
        if out and out[-1][1] + out[-1][2] == s:
            out[-1] = (out[-1][0], out[-1][1], out[-1][2] + 1)
        else:
            out.append((i, s, 1))
    return out


def view(q, p, a, kind):
    return q[:, a:a + CAP].bitcast(dt.uint8) if kind == "codes" else p[:, a:a + CAP]


def write(topo, core, engines, src, dst, arrived):
    rid, pid, _ = topo.addr(core)
    return RemoteDMATransfer(dst_ids=[DstId(rid=rid, pnc=pid)], dma_engine_mask=sum(1 << e for e in engines),
                             remote_sem=arrived, src=src, dst=dst)


def deliver(T, topo, r, name, engines, src, kind):
    d = pieces(T, topo, r)[name]
    came = senders(T, topo, d)
    dst = view(T.aq, T.ap, CAP * (came["early"] + came["late"]).index(r), kind)
    return write(topo, T.cores[d], engines, src, dst, T.sem.late if name in LATE else T.sem.early)


def helper_program(g, core, T, topo, r, name):
    out, local = topo.engines(core, T.cores[pieces(T, topo, r)[name]]), 0
    for kind, parts in CALLS:
        for piece, _, a, b, step in parts:
            if piece == name:
                engines = out[HELPER[kind]]
                g.wait_ge(T.sem[kind], len(range(a, b, step)))
                g.remote_dma_fused([deliver(T, topo, r, name, engines, view(T.rq, T.rp, 0, kind), kind)], local_sem=T.sem.loc)
                local += len(engines)
    g.wait_ge(T.sem.loc, local)


def rank_program(g, core, T, topo):
    r = T.rank_of(core)
    if r is None:
        for s in range(len(T.cores)):
            for name, c in helpers(T, topo, s).items():
                if c == core:
                    helper_program(g, core, T, topo, s, name)
        return
    sem = T.sem
    V, S, P, Y = g.vector, g.scalar, g.tensor, g.sync
    queue = {"V": V, "S": S, "P": P, "Y": Y, "G": g}
    Copy = ActivationFunctionType.Copy
    cnt = {"cv": 0, "cs": 0, "ct": 0}
    seen = {}

    def wait(name, s, n):
        if seen.get((name, s), 0) < n:
            queue[name].wait_ge(sem[s], n)
            seen[(name, s)] = n

    def inc(s, call):
        call.then_inc(sem[s], 1)
        cnt[s] += 1
        return s, cnt[s]

    to, helper, came = pieces(T, topo, r), helpers(T, topo, r), senders(T, topo, r)
    came["all"] = came["early"] + came["late"]
    names = [name for block, _ in BLOCKS for name in sorted(block, key=to.get)]
    done = {}

    for i, q in enumerate((Y, S)):
        q.dma_start(T.ls[16 * i:16 * i + 16, :], T.send[:, :]).then_inc(sem.sl, 16)
    Y.dma_start(T.xt[:, :], T.x[:, :]).then_inc(sem.sx, 16)
    for i in range(2):
        Y.dma_start(T.lm[16 * i:16 * i + 16, :], T.mp[:, :]).then_inc(sem.sm, 16)
    for i, maps in enumerate(WPARTS):
        a, b = 512 * maps[0], 512 * (maps[-1] + 1)
        Y.dma_start(T.wt[:, a:b], T.w[:, a:b]).then_inc(sem["sw%d" % i], 16)

    inc("cv", V.memset(T.win[:, 0:STRIDE * MAPS:STRIDE], 0.0))
    for k in range(MAPS):
        o = k * STRIDE + 1 + COLS + CAP * r
        zeros = inc("cv", V.memset(T.win[:, o:o + CAP], 0.0))

    wait("V", "sl", 32)
    for i, d, n in runs([to[name] for name in names]):
        offs = inc("cv", V.tensor_scalar(T.offs[0:32, 4 * i:4 * (i + n)], T.ls[0:32, 4 * d:4 * (d + n)], 4.0, 0.0,
                                         AluOpType.mult, AluOpType.max))
    wait("V", *offs)
    for p in (32, 64, 96):
        offs = inc("cv", V.tensor_copy(T.offs[p:p + 32, 0:28], T.offs[0:32, 0:28]))

    def span(b):
        lo = CAP * sum(len(block) for block, _ in BLOCKS[:b])
        return lo, lo + CAP * len(BLOCKS[b][0])

    def gather(b):
        lo, hi = span(b)
        done["rows", b] = []
        for t, name in enumerate(BLOCKS[b][1]):
            wait(name, *offs)
            wait(name, "sx", 16)
            out = T.h[:, 4 * lo + t:4 * hi:4]
            src = T.xt[:, t:4 * COLS].indirect(T.offs[:, lo // 16:hi // 16])
            done["rows", b].append(inc("cv", V.tensor_copy(out, src)) if name == "V"
                                   else inc("cs", S.activation(out, src, Copy)))

    def pack(b):
        lo, hi = span(b)
        for rows in done["rows", b]:
            wait("V", *rows)
        n = inc("cv", V.quantize_mx(T.hq[:, lo:hi], T.hp[:, lo:hi], T.h[:, 4 * lo:4 * hi]))
        done.update({name: n for name in BLOCKS[b][0]})

    def pack_w(i):
        a, b = WPARTS[i][0], WPARTS[i][-1] + 1
        wait("V", "sw%d" % i, 16)
        n = inc("cv", V.quantize_mx(T.wq[:, 128 * a:128 * b], T.wp[:, 128 * a:128 * b], T.wt[:, 512 * a:512 * b]))
        done.update({("w", k): n for k in WPARTS[i]})

    out = topo.engines(core, T.cores[to["f1a"]])
    comes = {"early": 0, "late": 0}
    for kind, parts in CALLS:
        for name, _, a, b, step in parts:
            comes["late" if name in LATE else "early"] += len(out[HELPER[kind]] if name in RELAYED else out[a:b:step])

    full = {k: [zeros] for k in range(MAPS)}
    banks = []

    def fill(what, k, name):
        bank = len(banks) % MAPS
        if len(banks) >= MAPS:
            wait("P", *banks[len(banks) - MAPS])
        wait("P", *done["w", k])
        if what == "x":
            wait("P", *done["x"])
            q, p, a, b, cuts = T.xq, T.xp, 0, COLS, [(0, 1, COLS)]
        else:
            for arr in ("early", "late"):
                if what in (arr, "all"):
                    wait("P", arr, comes[arr])
            a = CAP * came["all"].index(came[what][0])
            q, p, b = T.aq, T.ap, a + CAP * len(came[what])
            cuts = [(CAP * i, 1 + COLS + CAP * s, CAP * n) for i, s, n in runs(came[what])]
        w = slice(128 * k, 128 * k + 128)
        m = inc("ct", P.matmul_mx(T.ps[:, 512 * bank:512 * bank + b - a], T.wq[:, w], T.wp[:, w],
                                  q[:, a:b], p[:, a:b], True, True))
        wait(name, *m)
        for a, at, n in cuts:
            dst, src = T.win[:, k * STRIDE + at:k * STRIDE + at + n], T.ps[:, 512 * bank + a:512 * bank + a + n]
            last = inc("cv", V.tensor_copy(dst, src)) if name == "V" else inc("cs", S.activation(dst, src, Copy))
        full[k].append(last)
        banks.append(last)

    def pick(name, k, a, b):
        wait(name, *done["offm"])
        for need in full[k]:
            wait(name, *need)
        return T.win[:, k * STRIDE:k * STRIDE + WIN].indirect(T.offm[:, 32 * k + a // 16:32 * k + b // 16])

    def summed(name, a, b):
        for c in range(a, b, 128):
            wait(name, *done["sum", c])

    stores = 0

    gather(0)
    pack(0)
    for step in PLAN:
        if step[0] == "gather":
            gather(step[1])
        elif step[0] == "pack":
            pack(step[1])
        elif step == ("x",):
            done["x"] = inc("cv", V.quantize_mx(T.xq[:, :], T.xp[:, :], T.xt[:, :]))
        elif step[0] == "w":
            pack_w(step[1])
        elif step[0] == "offm":
            n = step[1]
            if n == 0:
                wait("V", "sm", 32)
                done["offm"] = inc("cv", V.tensor_scalar(T.offm[0:32, :], T.lm[0:32, :], 1.0, None, AluOpType.add))
            else:
                wait("V", *done["offm"])
                done["offm"] = inc("cv", V.tensor_copy(T.offm[n:2 * n, :], T.offm[0:n, :]))
        elif step[0] == "pick":
            _, k, a, b = step
            last = inc("cs", S.activation(T.g0[:, a:b], pick("S", k, a, b), Copy))
            done.update({("sum", c): last for c in range(a, b, 128)})
        elif step[0] == "add":
            _, k, a, b = step
            other = T.g0 if done["sum", a][0] == "cs" else T.acc
            summed("V", a, b)
            last = inc("cv", V.tensor_tensor(T.acc[:, a:b], pick("V", k, a, b), other[:, a:b], AluOpType.add))
            done.update({("sum", c): last for c in range(a, b, 128)})
        elif step[0] == "store":
            _, name, a, b = step
            summed(name, a, b)
            queue[name].dma_start(T.y[:, a:b], T.acc[:, a:b]).then_inc(sem.sy, 16)
            stores += 16
        else:
            fill(*step)

    sets = {"out": out, "home": [e for e in topo.engines(core, T.cores[to["m"]]) if e not in out]}
    local = 0
    for kind, parts in CALLS:
        transfers = []
        for name, which, a, b, step in parts:
            wait("G", *done[name])
            engines, src = sets[which][a:b:step], view(T.hq, T.hp, CAP * names.index(name), kind)
            local += len(engines)
            if name in RELAYED:
                transfers.append(write(topo, helper[name], engines, src, view(T.rq, T.rp, 0, kind), sem[kind]))
            else:
                transfers.append(deliver(T, topo, r, name, engines, src, kind))
        g.remote_dma_fused(transfers, local_sem=sem.loc)
    wait("G", "loc", local)
    Y.wait_ge(sem.sy, stores)
